import numpy as np
import ml_dtypes


def mxq(x, axis, fmt="e4m3"):
    dtype, down = {"e4m3": (ml_dtypes.float8_e4m3fn, 7), "e5m2": (ml_dtypes.float8_e5m2, 14)}[fmt]
    v = np.moveaxis(np.asarray(x, np.float32).astype(ml_dtypes.bfloat16).astype(np.float64), axis, -1)
    blocks = v.reshape(v.shape[:-1] + (-1, 32))
    amax = np.abs(blocks).max(-1, keepdims=True)
    byte = np.maximum(np.where(amax > 0, np.frexp(amax)[1] - 1 + 127, 0) - down, 1)
    scale = np.exp2(byte - 127.0)
    codes = (blocks / scale).astype(np.float32).astype(dtype).astype(np.float64)
    return np.moveaxis((codes * scale).reshape(v.shape), -1, axis)


WIDE = False


def mx_kscale(k):
    if not WIDE:
        return np.ones(k)
    levels = np.array([10, -10, 5, -5, 0])
    if k % 512:
        return np.exp2(np.random.permutation(np.resize(levels, k // 32))).repeat(32)
    a = np.empty((k // 512, 16))
    for p in range(k // 512):
        a[p, :8] = np.random.permutation(np.resize(levels, 8))
        for g in range(8):
            far = levels[np.abs(levels - a[p, g]) >= 10]
            a[p, g + 8] = far[np.random.randint(len(far))]
    return np.exp2(a.ravel()).repeat(32)


def f64(x):
    return np.asarray(x).astype(np.float64)


E2M1 = np.array([0.0, 0.5, 1.0, 1.5, 2.0, 3.0, 4.0, 6.0, -0.0, -0.5, -1.0, -1.5, -2.0, -3.0, -4.0, -6.0])


def pack_weight(w, fmt):
    k, n = w.shape
    w = f64(np.asarray(w, np.float32).astype(ml_dtypes.bfloat16)).reshape(k // 32, 32, n)
    amax = np.abs(w).max(1)
    if fmt == "e4m3":
        byte = np.frexp(amax)[1] - 1 + 127 - 7
    else:
        mant, ex = np.frexp(amax / 6.0)
        byte = np.where(mant > 0.5, ex, ex - 1) + 127
    byte = np.clip(np.where(amax > 0, byte, 1), 1, 254)
    scaled = (w * np.exp2(127.0 - byte)[:, None, :]).reshape(k, n).astype(np.float32)
    by_word = np.ascontiguousarray(scaled.reshape(k // 512, 128, 4, n).transpose(0, 1, 3, 2))
    if fmt == "e4m3":
        words = by_word.astype(ml_dtypes.float8_e4m3fn).view(np.uint8)
    else:
        c = by_word.astype(ml_dtypes.float4_e2m1fn).view(np.uint8) & 0xF
        words = (c[..., 0::2] | (c[..., 1::2] << 4)).reshape(k // 512, 128, 2 * n)
    return np.ascontiguousarray(words), np.ascontiguousarray(byte.astype(np.uint8).reshape(k // 512, 16, n))


def unpack_weight(words, scales, fmt):
    g, _, n = scales.shape
    words = np.ascontiguousarray(words).reshape(g, 128, n, -1)
    if fmt == "e4m3":
        vals = words.view(ml_dtypes.float8_e4m3fn).astype(np.float64)
    else:
        nib = np.empty((g, 128, n, 4), np.uint8)
        nib[..., 0::2] = words & 0xF
        nib[..., 1::2] = words >> 4
        vals = E2M1[nib]
    vals = vals * np.repeat(np.exp2(scales.astype(np.float64) - 127.0), 8, axis=1)[..., None]
    return vals.transpose(0, 1, 3, 2).reshape(g * 512, n)


K, L, T, N = 1024, 1024, 512, 512


def setup_inputs():
    n = np.random.standard_normal
    fk = mx_kscale(K)
    fl = mx_kscale(L)
    xtp = pack_weight(n((K, T)) / fk[:, None], "e4m3")
    xqp = pack_weight(n((L, T)) / fl[:, None], "e2m1")
    wqp = pack_weight(n((L, N)) * 1 / np.sqrt(L) * fl[:, None], "e4m3")
    wbp = pack_weight(n((K, N)) * 1 / np.sqrt(K) * fk[:, None], "e2m1")
    wcp = pack_weight(n((L, N)) * 1 / np.sqrt(L) * fl[:, None], "e4m3")
    return {
        "xt_words": xtp[0],
        "xt_scales": xtp[1],
        "wa": (n((K, N)) * 1 / np.sqrt(K) * fk[:, None]).astype(np.float32),
        "xq_words": xqp[0],
        "xq_scales": xqp[1],
        "wq_words": wqp[0],
        "wq_scales": wqp[1],
        "wb_words": wbp[0],
        "wb_scales": wbp[1],
        "wc_words": wcp[0],
        "wc_scales": wcp[1],
    }


def reference(xt_words, xt_scales, wa, xq_words, xq_scales, wq_words, wq_scales, wb_words, wb_scales, wc_words, wc_scales):
    xtu = unpack_weight(xt_words, xt_scales, "e4m3")
    xqu = unpack_weight(xq_words, xq_scales, "e2m1")
    wqu = unpack_weight(wq_words, wq_scales, "e4m3")
    wbu = unpack_weight(wb_words, wb_scales, "e2m1")
    wcu = unpack_weight(wc_words, wc_scales, "e4m3")
    waq = mxq(f64(wa), 0, "e4m3")
    p = waq.T @ xtu + wqu.T @ xqu
    r = wbu.T @ xtu
    s = wcu.T @ xqu
    lo = np.minimum(r, s)
    hi = np.maximum(r, s)
    y = np.maximum(lo, np.minimum(hi, 0.7 * p))
    return y

@@ -1,0 +1,200 @@
+from contextlib import ExitStack
+
+import concourse.mybir as mybir
+
+K, L, T, N = 1024, 1024, 512, 512
+FLOPS = 2 * T * N * (2 * K + 2 * L)
+
+F32 = mybir.dt.float32
+BF16 = mybir.dt.bfloat16
+I32 = mybir.dt.int32
+U32 = mybir.dt.uint32
+U8 = mybir.dt.uint8
+FP8X4 = mybir.dt.float8_e4m3fn_x4
+FP4X4 = mybir.dt.float4_e2m1fn_x4
+ALU = mybir.AluOpType
+
+P = 128
+PACK = 4
+K_PASS = P * PACK
+PASSES = K // K_PASS
+TILES = N // P
+HALF = N // 2
+
+
+def tile_mix_three_sums_middle_kernel(
+    tc, xt_words, xt_scales, wa, xq_words, xq_scales, wq_words, wq_scales,
+    wb_words, wb_scales, wc_words, wc_scales, out,
+):
+    nc = tc.nc
+    with ExitStack() as ctx:
+        keep = ctx.enter_context(tc.tile_pool(name="keep", bufs=1))
+        psum = ctx.enter_context(tc.psum_pool(name="psum", bufs=1))
+        ctx.enter_context(tc.manual_schedule())
+
+        def zeroed_plane(name):
+            plane = keep.tile([P, PASSES, 512], U8, name=name, align_bytes=64)
+            nc.vector.memset(plane[:].bitcast(I32), 0)
+            return plane
+
+        def load_scales(queue, plane, scales):
+            for r in range(4):
+                queue.dma_start(
+                    out=plane[r:P:32, :, :].bitcast(I32),
+                    in_=scales[:, r:16:4, :].rearrange("z q c -> q z c").bitcast(I32),
+                )
+
+        def load_fp8(name, words):
+            codes = keep.tile([P, PASSES, 512], U32, name=name, align_bytes=64)
+            nc.sync.dma_start(
+                out=codes[:].bitcast(I32),
+                in_=words.rearrange("z p c r -> p z (c r)").bitcast(I32),
+            )
+            return codes
+
+        def load_fp4(name, words):
+            codes = keep.tile([P, PASSES, 1024], U8, name=name, align_bytes=64)
+            nc.sync.dma_start(
+                out=codes[:].bitcast(I32),
+                in_=words.rearrange("z p b -> p z b").bitcast(I32),
+            )
+            return codes
+
+        def load_wa(h, z):
+            raw = keep.tile([P, PACK, HALF], F32, name="wa_raw%d%d" % (h, z))
+            rows = wa[z * K_PASS:(z + 1) * K_PASS, h * HALF:(h + 1) * HALF]
+            nc.sync.dma_start(out=raw[:], in_=rows.rearrange("(p j) n -> p j n", j=PACK))
+            return raw
+
+        planes = keep.tile([P, 4, PASSES, 512], U8, name="planes", align_bytes=64)
+        nc.vector.memset(planes[:].bitcast(I32), 0)
+        xt_s, wb_s, xq_s, wc_s = (planes[:, j, :, :] for j in range(4))
+        wq_s = zeroed_plane("wq_s")
+
+        staged = keep.tile([16, 4, PASSES, 512], U8, name="staged", align_bytes=64)
+        for j, scales in enumerate((xt_scales, wb_scales, xq_scales, wc_scales)):
+            nc.sync.dma_start(
+                out=staged[:, j, :, :].bitcast(I32),
+                in_=scales.rearrange("z q c -> q z c").bitcast(I32),
+            )
+        xt = load_fp8("xt", xt_words)
+        wb = load_fp4("wb", wb_words)
+        xq = load_fp4("xq", xq_words)
+        for r in range(4):
+            queue = nc.sync if r == 0 else nc.scalar
+            queue.dma_start(
+                out=planes[r:P:32].rearrange("q j z c -> q (j z c)").bitcast(I32),
+                in_=staged[r:16:4].rearrange("q j z c -> q (j z c)").bitcast(I32),
+            )
+        wc = load_fp8("wc", wc_words)
+        load_scales(nc.gpsimd, wq_s, wq_scales)
+        raw = {}
+        raw[0, 0] = load_wa(0, 0)
+        raw[0, 1] = load_wa(0, 1)
+        wq = load_fp8("wq", wq_words)
+        raw[1, 0] = load_wa(1, 0)
+        raw[1, 1] = load_wa(1, 1)
+
+        def mm(acc, lhsT, lhsT_scale, rhs, rhs_scale, start, stop):
+            nc.tensor.matmul_mx(out=acc[:], lhsT=lhsT, lhsT_scale=lhsT_scale, rhs=rhs,
+                                rhs_scale=rhs_scale, start=start, stop=stop)
+
+        r_sb, s_ps, p_ps, lo, hi, clipped = {}, {}, {}, {}, {}, {}
+        grouped, wa_codes, wa_s = {}, {}, {}
+
+        def product_r(i):
+            acc = psum.tile([P, T], F32, name="rp%d" % i)
+            for z in range(PASSES):
+                mm(acc, wb[:, z, 2 * P * i:2 * P * (i + 1)].bitcast(FP4X4), wb_s[:, z, P * i:P * (i + 1)],
+                   xt[:, z, :].bitcast(FP8X4), xt_s[:, z, :], z == 0, z == PASSES - 1)
+            r_sb[i] = keep.tile([P, T], F32, name="r%d" % i)
+            nc.scalar.copy(out=r_sb[i][:], in_=acc[:])
+
+        def product_s(i):
+            s_ps[i] = psum.tile([P, T], F32, name="s%d" % i)
+            for z in range(PASSES):
+                mm(s_ps[i], wc[:, z, P * i:P * (i + 1)].bitcast(FP8X4), wc_s[:, z, P * i:P * (i + 1)],
+                   xq[:, z, :].bitcast(FP4X4), xq_s[:, z, :], z == 0, z == PASSES - 1)
+
+        def bounds(i):
+            lo[i] = keep.tile([P, T], F32, name="lo%d" % i)
+            hi[i] = keep.tile([P, T], F32, name="hi%d" % i)
+            nc.vector.tensor_tensor(out=hi[i][:], in0=s_ps[i][:], in1=r_sb[i][:], op=ALU.max)
+            nc.vector.tensor_tensor(out=lo[i][:], in0=s_ps[i][:], in1=r_sb[i][:], op=ALU.min)
+
+        def open_p(i):
+            p_ps[i] = psum.tile([P, T], F32, name="rp%d" % i)
+            for z in range(PASSES):
+                mm(p_ps[i], wq[:, z, P * i:P * (i + 1)].bitcast(FP8X4), wq_s[:, z, P * i:P * (i + 1)],
+                   xq[:, z, :].bitcast(FP4X4), xq_s[:, z, :], z == 0, False)
+
+        def cast_wa(copy, h, z):
+            grouped[h, z] = keep.tile([P, HALF, PACK], BF16, name="wa_bf%d%d" % (h, z), align_bytes=64)
+            copy(
+                out=grouped[h, z][:].rearrange("p (c i) j -> p c j i", i=4),
+                in_=raw[h, z][:].rearrange("p j (c i) -> p c j i", i=4),
+            )
+
+        def quantize_wa(h, z):
+            wa_codes[h, z] = keep.tile([P, HALF], U32, name="wa_codes%d%d" % (h, z), align_bytes=64)
+            wa_s[h, z] = keep.tile([P, HALF], U8, name="wa_s%d%d" % (h, z), align_bytes=64)
+            nc.vector.quantize_mx(
+                out=wa_codes[h, z][:].bitcast(FP8X4),
+                scales=wa_s[h, z][:],
+                in_=grouped[h, z][:].rearrange("p c j -> p (c j)"),
+            )
+
+        def add_wa(i, z):
+            h, c0 = divmod(i * P, HALF)
+            mm(p_ps[i], wa_codes[h, z][:, c0:c0 + P].bitcast(FP8X4), wa_s[h, z][:, c0:c0 + P],
+               xt[:, z, :].bitcast(FP8X4), xt_s[:, z, :], False, z == PASSES - 1)
+
+        def clip_above(i):
+            clipped[i] = keep.tile([P, T], F32, name="clipped%d" % i)
+            nc.vector.scalar_tensor_tensor(out=clipped[i][:], in0=p_ps[i][:], scalar=0.7, in1=hi[i][:],
+                                           op0=ALU.mult, op1=ALU.min)
+
+        def finish(i, queue, t0, t1):
+            y = keep.tile([P, t1 - t0], F32, name="y%d_%d" % (i, t0))
+            nc.vector.tensor_tensor(out=y[:], in0=clipped[i][:, t0:t1], in1=lo[i][:, t0:t1], op=ALU.max)
+            queue.dma_start(out=out[i * P:(i + 1) * P, t0:t1], in_=y[:])
+
+        cast_wa(nc.vector.tensor_copy, 0, 0)
+        quantize_wa(0, 0)
+        product_r(0)
+        product_s(0)
+        bounds(0)
+        product_r(1)
+        product_s(1)
+        bounds(1)
+        cast_wa(nc.scalar.copy, 0, 1)
+        product_r(2)
+        product_s(2)
+        bounds(2)
+        quantize_wa(0, 1)
+        product_r(3)
+        product_s(3)
+        bounds(3)
+        cast_wa(nc.scalar.copy, 1, 0)
+        cast_wa(nc.scalar.copy, 1, 1)
+        for i in (0, 1):
+            open_p(i)
+            add_wa(i, 0)
+            add_wa(i, 1)
+        open_p(2)
+        open_p(3)
+        clip_above(0)
+        quantize_wa(1, 0)
+        clip_above(1)
+        finish(0, nc.sync, 0, T)
+        quantize_wa(1, 1)
+        finish(1, nc.sync, 0, T)
+        add_wa(2, 0)
+        add_wa(3, 0)
+        add_wa(2, 1)
+        add_wa(3, 1)
+        clip_above(2)
+        clip_above(3)
+        finish(2, nc.sync, 0, T)
+        finish(3, nc.scalar, 0, T // 2)
+        finish(3, nc.sync, T // 2, T)

@@ -18,7 +18,6 @@ P = 128
 PACK = 4
 K_PASS = P * PACK
 PASSES = K // K_PASS
-TILES = N // P
 HALF = N // 2
 
 
@@ -32,23 +31,11 @@ def tile_mix_three_sums_middle_kernel(
         psum = ctx.enter_context(tc.psum_pool(name="psum", bufs=1))
         ctx.enter_context(tc.manual_schedule())
 
-        def zeroed_plane(name):
-            plane = keep.tile([P, PASSES, 512], U8, name=name, align_bytes=64)
-            nc.vector.memset(plane[:].bitcast(I32), 0)
-            return plane
-
-        def load_scales(queue, plane, scales):
-            for r in range(4):
-                queue.dma_start(
-                    out=plane[r:P:32, :, :].bitcast(I32),
-                    in_=scales[:, r:16:4, :].rearrange("z q c -> q z c").bitcast(I32),
-                )
-
-        def load_fp8(name, words):
-            codes = keep.tile([P, PASSES, 512], U32, name=name, align_bytes=64)
+        def load_fp8(name, words, c0, c1):
+            codes = keep.tile([P, PASSES, c1 - c0], U32, name=name, align_bytes=64)
             nc.sync.dma_start(
                 out=codes[:].bitcast(I32),
-                in_=words.rearrange("z p c r -> p z (c r)").bitcast(I32),
+                in_=words[:, :, c0:c1, :].rearrange("z p c r -> p z (c r)").bitcast(I32),
             )
             return codes
 
@@ -66,41 +53,57 @@ def tile_mix_three_sums_middle_kernel(
             nc.sync.dma_start(out=raw[:], in_=rows.rearrange("(p j) n -> p j n", j=PACK))
             return raw
 
+        staged = keep.tile([P, 4, PASSES, 512], U8, name="staged", align_bytes=64)
+        nc.vector.memset(staged[:, 3, 0, :].bitcast(I32), 0)
         planes = keep.tile([P, 4, PASSES, 512], U8, name="planes", align_bytes=64)
         nc.vector.memset(planes[:].bitcast(I32), 0)
         xt_s, wb_s, xq_s, wc_s = (planes[:, j, :, :] for j in range(4))
-        wq_s = zeroed_plane("wq_s")
+        wq_s = keep.tile([P, PASSES, 512], U8, name="wq_s", align_bytes=64)
+        nc.vector.memset(wq_s[:].bitcast(I32), 0)
 
-        staged = keep.tile([16, 4, PASSES, 512], U8, name="staged", align_bytes=64)
         for j, scales in enumerate((xt_scales, wb_scales, xq_scales, wc_scales)):
-            nc.sync.dma_start(
-                out=staged[:, j, :, :].bitcast(I32),
+            queue = nc.scalar if j == 3 else nc.sync
+            queue.dma_start(
+                out=staged[0:16, j, :, :].bitcast(I32),
                 in_=scales.rearrange("z q c -> q z c").bitcast(I32),
             )
-        xt = load_fp8("xt", xt_words)
+        xt = load_fp8("xt", xt_words, 0, T)
         wb = load_fp4("wb", wb_words)
-        xq = load_fp4("xq", xq_words)
         for r in range(4):
-            queue = nc.sync if r == 0 else nc.scalar
+            queue = nc.sync if r < 2 else nc.scalar
             queue.dma_start(
                 out=planes[r:P:32].rearrange("q j z c -> q (j z c)").bitcast(I32),
                 in_=staged[r:16:4].rearrange("q j z c -> q (j z c)").bitcast(I32),
             )
-        wc = load_fp8("wc", wc_words)
-        load_scales(nc.gpsimd, wq_s, wq_scales)
-        raw = {}
-        raw[0, 0] = load_wa(0, 0)
-        raw[0, 1] = load_wa(0, 1)
-        wq = load_fp8("wq", wq_words)
-        raw[1, 0] = load_wa(1, 0)
-        raw[1, 1] = load_wa(1, 1)
+        xq = load_fp4("xq", xq_words)
+        wc = [load_fp8("wc%d" % h, wc_words, h * HALF, (h + 1) * HALF) for h in range(2)]
+        for r in range(4):
+            nc.gpsimd.dma_start(
+                out=wq_s[r:P:32, :, :].bitcast(I32),
+                in_=wq_scales[:, r:16:4, :].rearrange("z q c -> q z c").bitcast(I32),
+            )
+        raw, wq = {}, {}
+        for h in range(2):
+            raw[h, 0] = load_wa(h, 0)
+            raw[h, 1] = load_wa(h, 1)
+            wq[h] = load_fp8("wq%d" % h, wq_words, h * HALF, (h + 1) * HALF)
 
         def mm(acc, lhsT, lhsT_scale, rhs, rhs_scale, start, stop):
             nc.tensor.matmul_mx(out=acc[:], lhsT=lhsT, lhsT_scale=lhsT_scale, rhs=rhs,
                                 rhs_scale=rhs_scale, start=start, stop=stop)
 
+        warm = psum.tile([P, T], F32, name="s3")
+        for n in range(4):
+            mm(warm, xt[:, 0, 0:P].bitcast(FP8X4), staged[:, 3, 0, 0:P], xt[:, 0, :].bitcast(FP8X4),
+               staged[:, 3, 0, :], n == 0, n == 3)
+
         r_sb, s_ps, p_ps, lo, hi, clipped = {}, {}, {}, {}, {}, {}
         grouped, wa_codes, wa_s = {}, {}, {}
+        for h in range(2):
+            for z in range(PASSES):
+                grouped[h, z] = keep.tile([P, HALF, PACK], BF16, name="wa_bf%d%d" % (h, z), align_bytes=64)
+                wa_codes[h, z] = keep.tile([P, HALF], U32, name="wa_codes%d%d" % (h, z), align_bytes=64)
+                wa_s[h, z] = keep.tile([P, HALF], U8, name="wa_s%d%d" % (h, z), align_bytes=64)
 
         def product_r(i):
             acc = psum.tile([P, T], F32, name="rp%d" % i)
@@ -111,9 +114,10 @@ def tile_mix_three_sums_middle_kernel(
             nc.scalar.copy(out=r_sb[i][:], in_=acc[:])
 
         def product_s(i):
+            h, c0 = divmod(i * P, HALF)
             s_ps[i] = psum.tile([P, T], F32, name="s%d" % i)
             for z in range(PASSES):
-                mm(s_ps[i], wc[:, z, P * i:P * (i + 1)].bitcast(FP8X4), wc_s[:, z, P * i:P * (i + 1)],
+                mm(s_ps[i], wc[h][:, z, c0:c0 + P].bitcast(FP8X4), wc_s[:, z, P * i:P * (i + 1)],
                    xq[:, z, :].bitcast(FP4X4), xq_s[:, z, :], z == 0, z == PASSES - 1)
 
         def bounds(i):
@@ -123,25 +127,27 @@ def tile_mix_three_sums_middle_kernel(
             nc.vector.tensor_tensor(out=lo[i][:], in0=s_ps[i][:], in1=r_sb[i][:], op=ALU.min)
 
         def open_p(i):
+            h, c0 = divmod(i * P, HALF)
             p_ps[i] = psum.tile([P, T], F32, name="rp%d" % i)
             for z in range(PASSES):
-                mm(p_ps[i], wq[:, z, P * i:P * (i + 1)].bitcast(FP8X4), wq_s[:, z, P * i:P * (i + 1)],
+                mm(p_ps[i], wq[h][:, z, c0:c0 + P].bitcast(FP8X4), wq_s[:, z, P * i:P * (i + 1)],
                    xq[:, z, :].bitcast(FP4X4), xq_s[:, z, :], z == 0, False)
 
-        def cast_wa(copy, h, z):
-            grouped[h, z] = keep.tile([P, HALF, PACK], BF16, name="wa_bf%d%d" % (h, z), align_bytes=64)
-            copy(
-                out=grouped[h, z][:].rearrange("p (c i) j -> p c j i", i=4),
-                in_=raw[h, z][:].rearrange("p j (c i) -> p c j i", i=4),
+        def cast_wa(i, z, tiles=1):
+            h, c0 = divmod(i * P, HALF)
+            cols = slice(c0, c0 + tiles * P)
+            nc.scalar.copy(
+                out=grouped[h, z][:, cols, :].rearrange("p (c i) j -> p c j i", i=4),
+                in_=raw[h, z][:, :, cols].rearrange("p j (c i) -> p c j i", i=4),
             )
 
-        def quantize_wa(h, z):
-            wa_codes[h, z] = keep.tile([P, HALF], U32, name="wa_codes%d%d" % (h, z), align_bytes=64)
-            wa_s[h, z] = keep.tile([P, HALF], U8, name="wa_s%d%d" % (h, z), align_bytes=64)
+        def quantize_wa(i, z, tiles=1):
+            h, c0 = divmod(i * P, HALF)
+            cols = slice(c0, c0 + tiles * P)
             nc.vector.quantize_mx(
-                out=wa_codes[h, z][:].bitcast(FP8X4),
-                scales=wa_s[h, z][:],
-                in_=grouped[h, z][:].rearrange("p c j -> p (c j)"),
+                out=wa_codes[h, z][:, cols].bitcast(FP8X4),
+                scales=wa_s[h, z][:, cols],
+                in_=grouped[h, z][:, cols, :].rearrange("p c j -> p (c j)"),
             )
 
         def add_wa(i, z):
@@ -159,40 +165,44 @@ def tile_mix_three_sums_middle_kernel(
             nc.vector.tensor_tensor(out=y[:], in0=clipped[i][:, t0:t1], in1=lo[i][:, t0:t1], op=ALU.max)
             queue.dma_start(out=out[i * P:(i + 1) * P, t0:t1], in_=y[:])
 
-        cast_wa(nc.vector.tensor_copy, 0, 0)
-        quantize_wa(0, 0)
         product_r(0)
+        product_r(1)
         product_s(0)
         bounds(0)
-        product_r(1)
         product_s(1)
         bounds(1)
-        cast_wa(nc.scalar.copy, 0, 1)
+        cast_wa(0, 0)
+        quantize_wa(0, 0)
         product_r(2)
         product_s(2)
         bounds(2)
+        cast_wa(0, 1)
         quantize_wa(0, 1)
         product_r(3)
         product_s(3)
         bounds(3)
-        cast_wa(nc.scalar.copy, 1, 0)
-        cast_wa(nc.scalar.copy, 1, 1)
+        cast_wa(1, 0)
+        cast_wa(1, 1)
+        quantize_wa(1, 0)
+        quantize_wa(1, 1)
+        cast_wa(2, 0, tiles=2)
+        cast_wa(2, 1)
+        cast_wa(3, 1)
         for i in (0, 1):
             open_p(i)
             add_wa(i, 0)
             add_wa(i, 1)
-        open_p(2)
-        open_p(3)
         clip_above(0)
-        quantize_wa(1, 0)
         clip_above(1)
         finish(0, nc.sync, 0, T)
-        quantize_wa(1, 1)
+        quantize_wa(2, 0, tiles=2)
+        quantize_wa(2, 1)
         finish(1, nc.sync, 0, T)
-        add_wa(2, 0)
-        add_wa(3, 0)
-        add_wa(2, 1)
-        add_wa(3, 1)
+        quantize_wa(3, 1)
+        for i in (2, 3):
+            open_p(i)
+            add_wa(i, 0)
+            add_wa(i, 1)
         clip_above(2)
         clip_above(3)
         finish(2, nc.sync, 0, T)

@@ -39,11 +39,11 @@ def tile_mix_three_sums_middle_kernel(
             )
             return codes
 
-        def load_fp4(name, words):
-            codes = keep.tile([P, PASSES, 1024], U8, name=name, align_bytes=64)
+        def load_fp4(name, words, c0, c1):
+            codes = keep.tile([P, PASSES, 2 * (c1 - c0)], U8, name=name, align_bytes=64)
             nc.sync.dma_start(
                 out=codes[:].bitcast(I32),
-                in_=words.rearrange("z p b -> p z b").bitcast(I32),
+                in_=words[:, :, 2 * c0:2 * c1].rearrange("z p b -> p z b").bitcast(I32),
             )
             return codes
 
@@ -64,29 +64,33 @@ def tile_mix_three_sums_middle_kernel(
         for j, scales in enumerate((xt_scales, wb_scales, xq_scales, wc_scales)):
             queue = nc.scalar if j == 3 else nc.sync
             queue.dma_start(
-                out=staged[0:16, j, :, :].bitcast(I32),
+                out=staged[4:P:8, j, :, :].bitcast(I32),
                 in_=scales.rearrange("z q c -> q z c").bitcast(I32),
             )
         xt = load_fp8("xt", xt_words, 0, T)
-        wb = load_fp4("wb", wb_words)
+        wb = [load_fp4("wb0", wb_words, 0, HALF)]
         for r in range(4):
             queue = nc.sync if r < 2 else nc.scalar
             queue.dma_start(
                 out=planes[r:P:32].rearrange("q j z c -> q (j z c)").bitcast(I32),
-                in_=staged[r:16:4].rearrange("q j z c -> q (j z c)").bitcast(I32),
+                in_=staged[8 * r + 4:P:32].rearrange("q j z c -> q (j z c)").bitcast(I32),
             )
-        xq = load_fp4("xq", xq_words)
-        wc = [load_fp8("wc%d" % h, wc_words, h * HALF, (h + 1) * HALF) for h in range(2)]
+        xq = load_fp4("xq", xq_words, 0, T)
+        wc = [load_fp8("wc0", wc_words, 0, HALF)]
+        wb.append(load_fp4("wb1", wb_words, HALF, N))
+        wc.append(load_fp8("wc1", wc_words, HALF, N))
+        raw, wq = {}, {}
+        raw[0, 0] = load_wa(0, 0)
         for r in range(4):
-            nc.gpsimd.dma_start(
+            nc.sync.dma_start(
                 out=wq_s[r:P:32, :, :].bitcast(I32),
                 in_=wq_scales[:, r:16:4, :].rearrange("z q c -> q z c").bitcast(I32),
             )
-        raw, wq = {}, {}
-        for h in range(2):
-            raw[h, 0] = load_wa(h, 0)
-            raw[h, 1] = load_wa(h, 1)
-            wq[h] = load_fp8("wq%d" % h, wq_words, h * HALF, (h + 1) * HALF)
+        raw[0, 1] = load_wa(0, 1)
+        wq[0] = load_fp8("wq0", wq_words, 0, HALF)
+        raw[1, 0] = load_wa(1, 0)
+        raw[1, 1] = load_wa(1, 1)
+        wq[1] = load_fp8("wq1", wq_words, HALF, N)
 
         def mm(acc, lhsT, lhsT_scale, rhs, rhs_scale, start, stop):
             nc.tensor.matmul_mx(out=acc[:], lhsT=lhsT, lhsT_scale=lhsT_scale, rhs=rhs,
@@ -106,9 +110,10 @@ def tile_mix_three_sums_middle_kernel(
                 wa_s[h, z] = keep.tile([P, HALF], U8, name="wa_s%d%d" % (h, z), align_bytes=64)
 
         def product_r(i):
+            h, c0 = divmod(i * P, HALF)
             acc = psum.tile([P, T], F32, name="rp%d" % i)
             for z in range(PASSES):
-                mm(acc, wb[:, z, 2 * P * i:2 * P * (i + 1)].bitcast(FP4X4), wb_s[:, z, P * i:P * (i + 1)],
+                mm(acc, wb[h][:, z, 2 * c0:2 * (c0 + P)].bitcast(FP4X4), wb_s[:, z, P * i:P * (i + 1)],
                    xt[:, z, :].bitcast(FP8X4), xt_s[:, z, :], z == 0, z == PASSES - 1)
             r_sb[i] = keep.tile([P, T], F32, name="r%d" % i)
             nc.scalar.copy(out=r_sb[i][:], in_=acc[:])
@@ -155,9 +160,11 @@ def tile_mix_three_sums_middle_kernel(
             mm(p_ps[i], wa_codes[h, z][:, c0:c0 + P].bitcast(FP8X4), wa_s[h, z][:, c0:c0 + P],
                xt[:, z, :].bitcast(FP8X4), xt_s[:, z, :], False, z == PASSES - 1)
 
-        def clip_above(i):
+        for i in range(4):
             clipped[i] = keep.tile([P, T], F32, name="clipped%d" % i)
-            nc.vector.scalar_tensor_tensor(out=clipped[i][:], in0=p_ps[i][:], scalar=0.7, in1=hi[i][:],
+
+        def clip_above(i, t0=0, t1=T):
+            nc.vector.scalar_tensor_tensor(out=clipped[i][:, t0:t1], in0=p_ps[i][:, t0:t1], scalar=0.7, in1=hi[i][:, t0:t1],
                                            op0=ALU.mult, op1=ALU.min)
 
         def finish(i, queue, t0, t1):
@@ -171,15 +178,15 @@ def tile_mix_three_sums_middle_kernel(
         bounds(0)
         product_s(1)
         bounds(1)
-        cast_wa(0, 0)
-        quantize_wa(0, 0)
         product_r(2)
         product_s(2)
         bounds(2)
-        cast_wa(0, 1)
-        quantize_wa(0, 1)
+        cast_wa(0, 0)
+        quantize_wa(0, 0)
         product_r(3)
         product_s(3)
+        cast_wa(0, 1)
+        quantize_wa(0, 1)
         bounds(3)
         cast_wa(1, 0)
         cast_wa(1, 1)
@@ -194,17 +201,20 @@ def tile_mix_three_sums_middle_kernel(
             add_wa(i, 1)
         clip_above(0)
         clip_above(1)
-        finish(0, nc.sync, 0, T)
         quantize_wa(2, 0, tiles=2)
+        finish(0, nc.sync, 0, T)
         quantize_wa(2, 1)
         finish(1, nc.sync, 0, T)
         quantize_wa(3, 1)
-        for i in (2, 3):
-            open_p(i)
-            add_wa(i, 0)
-            add_wa(i, 1)
+        open_p(2)
+        open_p(3)
+        add_wa(2, 0)
+        add_wa(3, 0)
+        add_wa(2, 1)
+        add_wa(3, 1)
         clip_above(2)
-        clip_above(3)
+        clip_above(3, 0, T // 2)
         finish(2, nc.sync, 0, T)
+        clip_above(3, T // 2, T)
         finish(3, nc.scalar, 0, T // 2)
         finish(3, nc.sync, T // 2, T)

@@ -18,7 +18,16 @@ P = 128
 PACK = 4
 K_PASS = P * PACK
 PASSES = K // K_PASS
+TILES = N // P
 HALF = N // 2
+COLS = 512
+QUADRANT = 32
+ROWS = 4
+BLOCKS = K_PASS // 32
+STAGE_STEP = P // BLOCKS
+LINE = 4
+P_FACTOR = 0.7
+WARM_PASSES = 3
 
 
 def tile_mix_three_sums_middle_kernel(
@@ -48,102 +57,99 @@ def tile_mix_three_sums_middle_kernel(
             return codes
 
         def load_wa(h, z):
-            raw = keep.tile([P, PACK, HALF], F32, name="wa_raw%d%d" % (h, z))
-            rows = wa[z * K_PASS:(z + 1) * K_PASS, h * HALF:(h + 1) * HALF]
-            nc.sync.dma_start(out=raw[:], in_=rows.rearrange("(p j) n -> p j n", j=PACK))
-            return raw
+            rows = keep.tile([P, PACK, HALF], F32, name="wa_rows%d%d" % (h, z))
+            source = wa[z * K_PASS:(z + 1) * K_PASS, h * HALF:(h + 1) * HALF]
+            nc.sync.dma_start(out=rows[:], in_=source.rearrange("(p j) c -> p j c", j=PACK))
+            return rows
 
-        staged = keep.tile([P, 4, PASSES, 512], U8, name="staged", align_bytes=64)
-        nc.vector.memset(staged[:, 3, 0, :].bitcast(I32), 0)
-        planes = keep.tile([P, 4, PASSES, 512], U8, name="planes", align_bytes=64)
+        def matmul(acc, lhsT, lhsT_scale, rhs, rhs_scale, start, stop):
+            nc.tensor.matmul_mx(out=acc[:], lhsT=lhsT, lhsT_scale=lhsT_scale, rhs=rhs,
+                                rhs_scale=rhs_scale, start=start, stop=stop)
+
+        early_scales = (xt_scales, wb_scales, xq_scales, wc_scales)
+        staged = keep.tile([P, len(early_scales), PASSES, COLS], U8, name="staged", align_bytes=64)
+        wq_plane = keep.tile([P, PASSES, COLS], U8, name="wq_plane", align_bytes=64)
+        nc.vector.memset(wq_plane[:].bitcast(I32), 0)
+        planes = keep.tile([P, len(early_scales), PASSES, COLS], U8, name="planes", align_bytes=64)
         nc.vector.memset(planes[:].bitcast(I32), 0)
-        xt_s, wb_s, xq_s, wc_s = (planes[:, j, :, :] for j in range(4))
-        wq_s = keep.tile([P, PASSES, 512], U8, name="wq_s", align_bytes=64)
-        nc.vector.memset(wq_s[:].bitcast(I32), 0)
+        xt_plane, wb_plane, xq_plane, wc_plane = (planes[:, o, :, :] for o in range(len(early_scales)))
 
-        for j, scales in enumerate((xt_scales, wb_scales, xq_scales, wc_scales)):
-            queue = nc.scalar if j == 3 else nc.sync
+        for queue, o in zip((nc.sync, nc.sync, nc.scalar, nc.scalar), range(len(early_scales))):
             queue.dma_start(
-                out=staged[4:P:8, j, :, :].bitcast(I32),
-                in_=scales.rearrange("z q c -> q z c").bitcast(I32),
+                out=staged[ROWS:P:STAGE_STEP, o, :, :].bitcast(I32),
+                in_=early_scales[o].rearrange("z q c -> q z c").bitcast(I32),
             )
+
+        def load_wq_scales(queue, r):
+            queue.dma_start(
+                out=wq_plane[r:P:QUADRANT, :, :].bitcast(I32),
+                in_=wq_scales[:, r:BLOCKS:ROWS, :].rearrange("z q c -> q z c").bitcast(I32),
+            )
+
+        load_wq_scales(nc.scalar, 0)
         xt = load_fp8("xt", xt_words, 0, T)
         wb = [load_fp4("wb0", wb_words, 0, HALF)]
-        for r in range(4):
-            queue = nc.sync if r < 2 else nc.scalar
+        for queue, r in zip((nc.sync, nc.sync, nc.scalar, nc.scalar), range(ROWS)):
             queue.dma_start(
-                out=planes[r:P:32].rearrange("q j z c -> q (j z c)").bitcast(I32),
-                in_=staged[8 * r + 4:P:32].rearrange("q j z c -> q (j z c)").bitcast(I32),
+                out=planes[r:P:QUADRANT].rearrange("q o z c -> q (o z c)").bitcast(I32),
+                in_=staged[STAGE_STEP * r + ROWS:P:QUADRANT].rearrange("q o z c -> q (o z c)").bitcast(I32),
             )
         xq = load_fp4("xq", xq_words, 0, T)
         wc = [load_fp8("wc0", wc_words, 0, HALF)]
         wb.append(load_fp4("wb1", wb_words, HALF, N))
         wc.append(load_fp8("wc1", wc_words, HALF, N))
-        raw, wq = {}, {}
-        raw[0, 0] = load_wa(0, 0)
-        for r in range(4):
-            nc.sync.dma_start(
-                out=wq_s[r:P:32, :, :].bitcast(I32),
-                in_=wq_scales[:, r:16:4, :].rearrange("z q c -> q z c").bitcast(I32),
-            )
-        raw[0, 1] = load_wa(0, 1)
+
+        warm = psum.tile([P, T], F32, name="s_bank%d" % (TILES - 1))
+        for n in range(WARM_PASSES):
+            matmul(warm, xt[:, 0, 0:P].bitcast(FP8X4), wq_plane[:, 0, 0:P], xt[:, 0, :].bitcast(FP8X4),
+                   wq_plane[:, 0, :], n == 0, n == WARM_PASSES - 1)
+
+        wa_rows, wq = {}, {}
+        wa_rows[0, 0] = load_wa(0, 0)
+        for r in range(1, ROWS):
+            load_wq_scales(nc.sync, r)
+        wa_rows[0, 1] = load_wa(0, 1)
         wq[0] = load_fp8("wq0", wq_words, 0, HALF)
-        raw[1, 0] = load_wa(1, 0)
-        raw[1, 1] = load_wa(1, 1)
+        wa_rows[1, 0] = load_wa(1, 0)
+        wa_rows[1, 1] = load_wa(1, 1)
         wq[1] = load_fp8("wq1", wq_words, HALF, N)
 
-        def mm(acc, lhsT, lhsT_scale, rhs, rhs_scale, start, stop):
-            nc.tensor.matmul_mx(out=acc[:], lhsT=lhsT, lhsT_scale=lhsT_scale, rhs=rhs,
-                                rhs_scale=rhs_scale, start=start, stop=stop)
-
-        warm = psum.tile([P, T], F32, name="s3")
-        for n in range(4):
-            mm(warm, xt[:, 0, 0:P].bitcast(FP8X4), staged[:, 3, 0, 0:P], xt[:, 0, :].bitcast(FP8X4),
-               staged[:, 3, 0, :], n == 0, n == 3)
-
-        r_sb, s_ps, p_ps, lo, hi, clipped = {}, {}, {}, {}, {}, {}
-        grouped, wa_codes, wa_s = {}, {}, {}
+        wa_bf16, wa_codes, wa_plane = {}, {}, {}
         for h in range(2):
             for z in range(PASSES):
-                grouped[h, z] = keep.tile([P, HALF, PACK], BF16, name="wa_bf%d%d" % (h, z), align_bytes=64)
+                wa_bf16[h, z] = keep.tile([P, HALF, PACK], BF16, name="wa_bf16_%d%d" % (h, z), align_bytes=64)
                 wa_codes[h, z] = keep.tile([P, HALF], U32, name="wa_codes%d%d" % (h, z), align_bytes=64)
-                wa_s[h, z] = keep.tile([P, HALF], U8, name="wa_s%d%d" % (h, z), align_bytes=64)
+                wa_plane[h, z] = keep.tile([P, HALF], U8, name="wa_plane%d%d" % (h, z), align_bytes=64)
+        r_sbuf, s_psum, p_psum, lo, hi, clipped = {}, {}, {}, {}, {}, {}
 
         def product_r(i):
             h, c0 = divmod(i * P, HALF)
-            acc = psum.tile([P, T], F32, name="rp%d" % i)
+            r_psum = psum.tile([P, T], F32, name="rp_bank%d" % i)
             for z in range(PASSES):
-                mm(acc, wb[h][:, z, 2 * c0:2 * (c0 + P)].bitcast(FP4X4), wb_s[:, z, P * i:P * (i + 1)],
-                   xt[:, z, :].bitcast(FP8X4), xt_s[:, z, :], z == 0, z == PASSES - 1)
-            r_sb[i] = keep.tile([P, T], F32, name="r%d" % i)
-            nc.scalar.copy(out=r_sb[i][:], in_=acc[:])
+                matmul(r_psum, wb[h][:, z, 2 * c0:2 * (c0 + P)].bitcast(FP4X4), wb_plane[:, z, P * i:P * (i + 1)],
+                       xt[:, z, :].bitcast(FP8X4), xt_plane[:, z, :], z == 0, z == PASSES - 1)
+            r_sbuf[i] = keep.tile([P, T], F32, name="r%d" % i)
+            nc.scalar.copy(out=r_sbuf[i][:], in_=r_psum[:])
 
         def product_s(i):
             h, c0 = divmod(i * P, HALF)
-            s_ps[i] = psum.tile([P, T], F32, name="s%d" % i)
+            s_psum[i] = psum.tile([P, T], F32, name="s_bank%d" % i)
             for z in range(PASSES):
-                mm(s_ps[i], wc[h][:, z, c0:c0 + P].bitcast(FP8X4), wc_s[:, z, P * i:P * (i + 1)],
-                   xq[:, z, :].bitcast(FP4X4), xq_s[:, z, :], z == 0, z == PASSES - 1)
+                matmul(s_psum[i], wc[h][:, z, c0:c0 + P].bitcast(FP8X4), wc_plane[:, z, P * i:P * (i + 1)],
+                       xq[:, z, :].bitcast(FP4X4), xq_plane[:, z, :], z == 0, z == PASSES - 1)
 
         def bounds(i):
             lo[i] = keep.tile([P, T], F32, name="lo%d" % i)
             hi[i] = keep.tile([P, T], F32, name="hi%d" % i)
-            nc.vector.tensor_tensor(out=hi[i][:], in0=s_ps[i][:], in1=r_sb[i][:], op=ALU.max)
-            nc.vector.tensor_tensor(out=lo[i][:], in0=s_ps[i][:], in1=r_sb[i][:], op=ALU.min)
+            nc.vector.tensor_tensor(out=hi[i][:], in0=s_psum[i][:], in1=r_sbuf[i][:], op=ALU.max)
+            nc.vector.tensor_tensor(out=lo[i][:], in0=s_psum[i][:], in1=r_sbuf[i][:], op=ALU.min)
 
-        def open_p(i):
-            h, c0 = divmod(i * P, HALF)
-            p_ps[i] = psum.tile([P, T], F32, name="rp%d" % i)
-            for z in range(PASSES):
-                mm(p_ps[i], wq[h][:, z, c0:c0 + P].bitcast(FP8X4), wq_s[:, z, P * i:P * (i + 1)],
-                   xq[:, z, :].bitcast(FP4X4), xq_s[:, z, :], z == 0, False)
-
-        def cast_wa(i, z, tiles=1):
+        def round_wa(i, z, tiles=1):
             h, c0 = divmod(i * P, HALF)
             cols = slice(c0, c0 + tiles * P)
             nc.scalar.copy(
-                out=grouped[h, z][:, cols, :].rearrange("p (c i) j -> p c j i", i=4),
-                in_=raw[h, z][:, :, cols].rearrange("p j (c i) -> p c j i", i=4),
+                out=wa_bf16[h, z][:, cols, :].rearrange("p (g e) j -> p g j e", e=LINE),
+                in_=wa_rows[h, z][:, :, cols].rearrange("p j (g e) -> p g j e", e=LINE),
             )
 
         def quantize_wa(i, z, tiles=1):
@@ -151,70 +157,82 @@ def tile_mix_three_sums_middle_kernel(
             cols = slice(c0, c0 + tiles * P)
             nc.vector.quantize_mx(
                 out=wa_codes[h, z][:, cols].bitcast(FP8X4),
-                scales=wa_s[h, z][:, cols],
-                in_=grouped[h, z][:, cols, :].rearrange("p c j -> p (c j)"),
+                scales=wa_plane[h, z][:, cols],
+                in_=wa_bf16[h, z][:, cols, :].rearrange("p c j -> p (c j)"),
             )
 
-        def add_wa(i, z):
-            h, c0 = divmod(i * P, HALF)
-            mm(p_ps[i], wa_codes[h, z][:, c0:c0 + P].bitcast(FP8X4), wa_s[h, z][:, c0:c0 + P],
-               xt[:, z, :].bitcast(FP8X4), xt_s[:, z, :], False, z == PASSES - 1)
+        def claim_p_bank(i):
+            p_psum[i] = psum.tile([P, T], F32, name="rp_bank%d" % i)
 
-        for i in range(4):
+        def add_wq(i, start=False):
+            h, c0 = divmod(i * P, HALF)
+            for z in range(PASSES):
+                matmul(p_psum[i], wq[h][:, z, c0:c0 + P].bitcast(FP8X4), wq_plane[:, z, P * i:P * (i + 1)],
+                       xq[:, z, :].bitcast(FP4X4), xq_plane[:, z, :], start and z == 0, False)
+
+        def add_wa(i, z, start=False):
+            h, c0 = divmod(i * P, HALF)
+            matmul(p_psum[i], wa_codes[h, z][:, c0:c0 + P].bitcast(FP8X4), wa_plane[h, z][:, c0:c0 + P],
+                   xt[:, z, :].bitcast(FP8X4), xt_plane[:, z, :], start, z == PASSES - 1)
+
+        for i in range(TILES):
             clipped[i] = keep.tile([P, T], F32, name="clipped%d" % i)
 
         def clip_above(i, t0=0, t1=T):
-            nc.vector.scalar_tensor_tensor(out=clipped[i][:, t0:t1], in0=p_ps[i][:, t0:t1], scalar=0.7, in1=hi[i][:, t0:t1],
-                                           op0=ALU.mult, op1=ALU.min)
+            nc.vector.scalar_tensor_tensor(
+                out=clipped[i][:, t0:t1], in0=p_psum[i][:, t0:t1], scalar=P_FACTOR, in1=hi[i][:, t0:t1],
+                op0=ALU.mult, op1=ALU.min,
+            )
 
-        def finish(i, queue, t0, t1):
-            y = keep.tile([P, t1 - t0], F32, name="y%d_%d" % (i, t0))
-            nc.vector.tensor_tensor(out=y[:], in0=clipped[i][:, t0:t1], in1=lo[i][:, t0:t1], op=ALU.max)
-            queue.dma_start(out=out[i * P:(i + 1) * P, t0:t1], in_=y[:])
+        def finish(i, queue, t0=0, t1=T):
+            middle = keep.tile([P, t1 - t0], F32, name="middle%d_%d" % (i, t0))
+            nc.vector.tensor_tensor(out=middle[:], in0=clipped[i][:, t0:t1], in1=lo[i][:, t0:t1], op=ALU.max)
+            queue.dma_start(out=out[i * P:(i + 1) * P, t0:t1], in_=middle[:])
 
-        product_r(0)
-        product_r(1)
-        product_s(0)
-        bounds(0)
-        product_s(1)
-        bounds(1)
-        product_r(2)
-        product_s(2)
-        bounds(2)
-        cast_wa(0, 0)
+        for i in range(TILES - 1):
+            product_r(i)
+            product_s(i)
+            bounds(i)
+        round_wa(0, 0)
         quantize_wa(0, 0)
-        product_r(3)
-        product_s(3)
-        cast_wa(0, 1)
+        product_r(TILES - 1)
+        product_s(TILES - 1)
+        bounds(TILES - 1)
+        round_wa(1, 0)
+        round_wa(0, 1)
+        round_wa(1, 1)
         quantize_wa(0, 1)
-        bounds(3)
-        cast_wa(1, 0)
-        cast_wa(1, 1)
         quantize_wa(1, 0)
         quantize_wa(1, 1)
-        cast_wa(2, 0, tiles=2)
-        cast_wa(2, 1)
-        cast_wa(3, 1)
-        for i in (0, 1):
-            open_p(i)
-            add_wa(i, 0)
-            add_wa(i, 1)
+        round_wa(2, 0, tiles=2)
+        round_wa(2, 1)
+        round_wa(3, 1)
+
+        claim_p_bank(0)
+        add_wq(0, start=True)
+        add_wa(0, 0)
+        claim_p_bank(1)
+        add_wq(1, start=True)
+        add_wa(0, 1)
+        add_wa(1, 0)
+        add_wa(1, 1)
         clip_above(0)
         clip_above(1)
         quantize_wa(2, 0, tiles=2)
-        finish(0, nc.sync, 0, T)
+        finish(0, nc.sync)
         quantize_wa(2, 1)
-        finish(1, nc.sync, 0, T)
+        finish(1, nc.sync)
         quantize_wa(3, 1)
-        open_p(2)
-        open_p(3)
-        add_wa(2, 0)
-        add_wa(3, 0)
-        add_wa(2, 1)
-        add_wa(3, 1)
+
+        for i in (2, 3):
+            claim_p_bank(i)
+            add_wa(i, 0, start=True)
+        for i in (2, 3):
+            add_wq(i)
+            add_wa(i, 1)
         clip_above(2)
         clip_above(3, 0, T // 2)
-        finish(2, nc.sync, 0, T)
+        finish(2, nc.sync)
         clip_above(3, T // 2, T)
         finish(3, nc.scalar, 0, T // 2)
         finish(3, nc.sync, T // 2, T)

from contextlib import ExitStack

import concourse.mybir as mybir

K, L, T, N = 1024, 1024, 512, 512
FLOPS = 2 * T * N * (2 * K + 2 * L)

F32 = mybir.dt.float32
BF16 = mybir.dt.bfloat16
I32 = mybir.dt.int32
U32 = mybir.dt.uint32
U8 = mybir.dt.uint8
FP8X4 = mybir.dt.float8_e4m3fn_x4
FP4X4 = mybir.dt.float4_e2m1fn_x4
ALU = mybir.AluOpType

P = 128
PACK = 4
K_PASS = P * PACK
PASSES = K // K_PASS
TILES = N // P
HALF = N // 2
COLS = 512
QUADRANT = 32
ROWS = 4
BLOCKS = K_PASS // 32
STAGE_STEP = P // BLOCKS
LINE = 4
P_FACTOR = 0.7
WARM_PASSES = 3


def tile_mix_three_sums_middle_kernel(
    tc, xt_words, xt_scales, wa, xq_words, xq_scales, wq_words, wq_scales,
    wb_words, wb_scales, wc_words, wc_scales, out,
):
    nc = tc.nc
    with ExitStack() as ctx:
        keep = ctx.enter_context(tc.tile_pool(name="keep", bufs=1))
        psum = ctx.enter_context(tc.psum_pool(name="psum", bufs=1))
        ctx.enter_context(tc.manual_schedule())

        def load_fp8(name, words, c0, c1):
            codes = keep.tile([P, PASSES, c1 - c0], U32, name=name, align_bytes=64)
            nc.sync.dma_start(
                out=codes[:].bitcast(I32),
                in_=words[:, :, c0:c1, :].rearrange("z p c r -> p z (c r)").bitcast(I32),
            )
            return codes

        def load_fp4(name, words, c0, c1):
            codes = keep.tile([P, PASSES, 2 * (c1 - c0)], U8, name=name, align_bytes=64)
            nc.sync.dma_start(
                out=codes[:].bitcast(I32),
                in_=words[:, :, 2 * c0:2 * c1].rearrange("z p b -> p z b").bitcast(I32),
            )
            return codes

        def load_wa(h, z):
            rows = keep.tile([P, PACK, HALF], F32, name="wa_rows%d%d" % (h, z))
            source = wa[z * K_PASS:(z + 1) * K_PASS, h * HALF:(h + 1) * HALF]
            nc.sync.dma_start(out=rows[:], in_=source.rearrange("(p j) c -> p j c", j=PACK))
            return rows

        def matmul(acc, lhsT, lhsT_scale, rhs, rhs_scale, start, stop):
            nc.tensor.matmul_mx(out=acc[:], lhsT=lhsT, lhsT_scale=lhsT_scale, rhs=rhs,
                                rhs_scale=rhs_scale, start=start, stop=stop)

        early_scales = (xt_scales, wb_scales, xq_scales, wc_scales)
        staged = keep.tile([P, len(early_scales), PASSES, COLS], U8, name="staged", align_bytes=64)
        wq_plane = keep.tile([P, PASSES, COLS], U8, name="wq_plane", align_bytes=64)
        nc.vector.memset(wq_plane[:].bitcast(I32), 0)
        planes = keep.tile([P, len(early_scales), PASSES, COLS], U8, name="planes", align_bytes=64)
        nc.vector.memset(planes[:].bitcast(I32), 0)
        xt_plane, wb_plane, xq_plane, wc_plane = (planes[:, o, :, :] for o in range(len(early_scales)))

        for queue, o in zip((nc.sync, nc.sync, nc.scalar, nc.scalar), range(len(early_scales))):
            queue.dma_start(
                out=staged[ROWS:P:STAGE_STEP, o, :, :].bitcast(I32),
                in_=early_scales[o].rearrange("z q c -> q z c").bitcast(I32),
            )

        def load_wq_scales(queue, r):
            queue.dma_start(
                out=wq_plane[r:P:QUADRANT, :, :].bitcast(I32),
                in_=wq_scales[:, r:BLOCKS:ROWS, :].rearrange("z q c -> q z c").bitcast(I32),
            )

        load_wq_scales(nc.scalar, 0)
        xt = load_fp8("xt", xt_words, 0, T)
        wb = [load_fp4("wb0", wb_words, 0, HALF)]
        for queue, r in zip((nc.sync, nc.sync, nc.scalar, nc.scalar), range(ROWS)):
            queue.dma_start(
                out=planes[r:P:QUADRANT].rearrange("q o z c -> q (o z c)").bitcast(I32),
                in_=staged[STAGE_STEP * r + ROWS:P:QUADRANT].rearrange("q o z c -> q (o z c)").bitcast(I32),
            )
        xq = load_fp4("xq", xq_words, 0, T)
        wc = [load_fp8("wc0", wc_words, 0, HALF)]
        wb.append(load_fp4("wb1", wb_words, HALF, N))
        wc.append(load_fp8("wc1", wc_words, HALF, N))

        warm = psum.tile([P, T], F32, name="s_bank%d" % (TILES - 1))
        for n in range(WARM_PASSES):
            matmul(warm, xt[:, 0, 0:P].bitcast(FP8X4), wq_plane[:, 0, 0:P], xt[:, 0, :].bitcast(FP8X4),
                   wq_plane[:, 0, :], n == 0, n == WARM_PASSES - 1)

        wa_rows, wq = {}, {}
        wa_rows[0, 0] = load_wa(0, 0)
        for r in range(1, ROWS):
            load_wq_scales(nc.sync, r)
        wa_rows[0, 1] = load_wa(0, 1)
        wq[0] = load_fp8("wq0", wq_words, 0, HALF)
        wa_rows[1, 0] = load_wa(1, 0)
        wa_rows[1, 1] = load_wa(1, 1)
        wq[1] = load_fp8("wq1", wq_words, HALF, N)

        wa_bf16, wa_codes, wa_plane = {}, {}, {}
        for h in range(2):
            for z in range(PASSES):
                wa_bf16[h, z] = keep.tile([P, HALF, PACK], BF16, name="wa_bf16_%d%d" % (h, z), align_bytes=64)
                wa_codes[h, z] = keep.tile([P, HALF], U32, name="wa_codes%d%d" % (h, z), align_bytes=64)
                wa_plane[h, z] = keep.tile([P, HALF], U8, name="wa_plane%d%d" % (h, z), align_bytes=64)
        r_sbuf, s_psum, p_psum, lo, hi, clipped = {}, {}, {}, {}, {}, {}

        def product_r(i):
            h, c0 = divmod(i * P, HALF)
            r_psum = psum.tile([P, T], F32, name="rp_bank%d" % i)
            for z in range(PASSES):
                matmul(r_psum, wb[h][:, z, 2 * c0:2 * (c0 + P)].bitcast(FP4X4), wb_plane[:, z, P * i:P * (i + 1)],
                       xt[:, z, :].bitcast(FP8X4), xt_plane[:, z, :], z == 0, z == PASSES - 1)
            r_sbuf[i] = keep.tile([P, T], F32, name="r%d" % i)
            nc.scalar.copy(out=r_sbuf[i][:], in_=r_psum[:])

        def product_s(i):
            h, c0 = divmod(i * P, HALF)
            s_psum[i] = psum.tile([P, T], F32, name="s_bank%d" % i)
            for z in range(PASSES):
                matmul(s_psum[i], wc[h][:, z, c0:c0 + P].bitcast(FP8X4), wc_plane[:, z, P * i:P * (i + 1)],
                       xq[:, z, :].bitcast(FP4X4), xq_plane[:, z, :], z == 0, z == PASSES - 1)

        def bounds(i):
            lo[i] = keep.tile([P, T], F32, name="lo%d" % i)
            hi[i] = keep.tile([P, T], F32, name="hi%d" % i)
            nc.vector.tensor_tensor(out=hi[i][:], in0=s_psum[i][:], in1=r_sbuf[i][:], op=ALU.max)
            nc.vector.tensor_tensor(out=lo[i][:], in0=s_psum[i][:], in1=r_sbuf[i][:], op=ALU.min)

        def round_wa(i, z, tiles=1):
            h, c0 = divmod(i * P, HALF)
            cols = slice(c0, c0 + tiles * P)
            nc.scalar.copy(
                out=wa_bf16[h, z][:, cols, :].rearrange("p (g e) j -> p g j e", e=LINE),
                in_=wa_rows[h, z][:, :, cols].rearrange("p j (g e) -> p g j e", e=LINE),
            )

        def quantize_wa(i, z, tiles=1):
            h, c0 = divmod(i * P, HALF)
            cols = slice(c0, c0 + tiles * P)
            nc.vector.quantize_mx(
                out=wa_codes[h, z][:, cols].bitcast(FP8X4),
                scales=wa_plane[h, z][:, cols],
                in_=wa_bf16[h, z][:, cols, :].rearrange("p c j -> p (c j)"),
            )

        def claim_p_bank(i):
            p_psum[i] = psum.tile([P, T], F32, name="rp_bank%d" % i)

        def add_wq(i, start=False):
            h, c0 = divmod(i * P, HALF)
            for z in range(PASSES):
                matmul(p_psum[i], wq[h][:, z, c0:c0 + P].bitcast(FP8X4), wq_plane[:, z, P * i:P * (i + 1)],
                       xq[:, z, :].bitcast(FP4X4), xq_plane[:, z, :], start and z == 0, False)

        def add_wa(i, z, start=False):
            h, c0 = divmod(i * P, HALF)
            matmul(p_psum[i], wa_codes[h, z][:, c0:c0 + P].bitcast(FP8X4), wa_plane[h, z][:, c0:c0 + P],
                   xt[:, z, :].bitcast(FP8X4), xt_plane[:, z, :], start, z == PASSES - 1)

        for i in range(TILES):
            clipped[i] = keep.tile([P, T], F32, name="clipped%d" % i)

        def clip_above(i, t0=0, t1=T):
            nc.vector.scalar_tensor_tensor(
                out=clipped[i][:, t0:t1], in0=p_psum[i][:, t0:t1], scalar=P_FACTOR, in1=hi[i][:, t0:t1],
                op0=ALU.mult, op1=ALU.min,
            )

        def finish(i, queue, t0=0, t1=T):
            middle = keep.tile([P, t1 - t0], F32, name="middle%d_%d" % (i, t0))
            nc.vector.tensor_tensor(out=middle[:], in0=clipped[i][:, t0:t1], in1=lo[i][:, t0:t1], op=ALU.max)
            queue.dma_start(out=out[i * P:(i + 1) * P, t0:t1], in_=middle[:])

        for i in range(TILES - 1):
            product_r(i)
            product_s(i)
            bounds(i)
        round_wa(0, 0)
        quantize_wa(0, 0)
        product_r(TILES - 1)
        product_s(TILES - 1)
        bounds(TILES - 1)
        round_wa(1, 0)
        round_wa(0, 1)
        round_wa(1, 1)
        quantize_wa(0, 1)
        quantize_wa(1, 0)
        quantize_wa(1, 1)
        round_wa(2, 0, tiles=2)
        round_wa(2, 1)
        round_wa(3, 1)

        claim_p_bank(0)
        add_wq(0, start=True)
        add_wa(0, 0)
        claim_p_bank(1)
        add_wq(1, start=True)
        add_wa(0, 1)
        add_wa(1, 0)
        add_wa(1, 1)
        clip_above(0)
        clip_above(1)
        quantize_wa(2, 0, tiles=2)
        finish(0, nc.sync)
        quantize_wa(2, 1)
        finish(1, nc.sync)
        quantize_wa(3, 1)

        for i in (2, 3):
            claim_p_bank(i)
            add_wa(i, 0, start=True)
        for i in (2, 3):
            add_wq(i)
            add_wa(i, 1)
        clip_above(2)
        clip_above(3, 0, T // 2)
        finish(2, nc.sync)
        clip_above(3, T // 2, T)
        finish(3, nc.scalar, 0, T // 2)
        finish(3, nc.sync, T // 2, T)
